import numpy as np
import ml_dtypes


def mxq(x, axis, fmt="e4m3"):
    dtype, down = {"e4m3": (ml_dtypes.float8_e4m3fn, 7), "e5m2": (ml_dtypes.float8_e5m2, 14)}[fmt]
    v = np.moveaxis(np.asarray(x, np.float32).astype(ml_dtypes.bfloat16).astype(np.float64), axis, -1)
    blocks = v.reshape(v.shape[:-1] + (-1, 32))
    amax = np.abs(blocks).max(-1, keepdims=True)
    byte = np.maximum(np.where(amax > 0, np.frexp(amax)[1] - 1 + 127, 0) - down, 1)
    scale = np.exp2(byte - 127.0)
    codes = (blocks / scale).astype(np.float32).astype(dtype).astype(np.float64)
    return np.moveaxis((codes * scale).reshape(v.shape), -1, axis)


WIDE = False


def mx_kscale(k):
    if not WIDE:
        return np.ones(k)
    levels = np.array([30, -30])
    if k % 512:
        return np.exp2(np.random.permutation(np.resize(levels, k // 32))).repeat(32)
    a = np.empty((k // 512, 16))
    for p in range(k // 512):
        a[p, :8] = np.random.permutation(np.resize(levels, 8))
        for g in range(8):
            far = levels[np.abs(levels - a[p, g]) >= 10]
            a[p, g + 8] = far[np.random.randint(len(far))]
    return np.exp2(a.ravel()).repeat(32)


def f64(x):
    return np.asarray(x).astype(np.float64)


E2M1 = np.array([0.0, 0.5, 1.0, 1.5, 2.0, 3.0, 4.0, 6.0, -0.0, -0.5, -1.0, -1.5, -2.0, -3.0, -4.0, -6.0])


def pack_weight(w, fmt):
    k, n = w.shape
    w = f64(np.asarray(w, np.float32).astype(ml_dtypes.bfloat16)).reshape(k // 32, 32, n)
    amax = np.abs(w).max(1)
    if fmt == "e4m3":
        byte = np.frexp(amax)[1] - 1 + 127 - 7
    else:
        mant, ex = np.frexp(amax / 6.0)
        byte = np.where(mant > 0.5, ex, ex - 1) + 127
    byte = np.clip(np.where(amax > 0, byte, 1), 1, 254)
    scaled = (w * np.exp2(127.0 - byte)[:, None, :]).reshape(k, n).astype(np.float32)
    by_word = np.ascontiguousarray(scaled.reshape(k // 512, 128, 4, n).transpose(0, 1, 3, 2))
    if fmt == "e4m3":
        words = by_word.astype(ml_dtypes.float8_e4m3fn).view(np.uint8)
    else:
        c = by_word.astype(ml_dtypes.float4_e2m1fn).view(np.uint8) & 0xF
        words = (c[..., 0::2] | (c[..., 1::2] << 4)).reshape(k // 512, 128, 2 * n)
    return np.ascontiguousarray(words), np.ascontiguousarray(byte.astype(np.uint8).reshape(k // 512, 16, n))


def unpack_weight(words, scales, fmt):
    g, _, n = scales.shape
    words = np.ascontiguousarray(words).reshape(g, 128, n, -1)
    if fmt == "e4m3":
        vals = words.view(ml_dtypes.float8_e4m3fn).astype(np.float64)
    else:
        nib = np.empty((g, 128, n, 4), np.uint8)
        nib[..., 0::2] = words & 0xF
        nib[..., 1::2] = words >> 4
        vals = E2M1[nib]
    vals = vals * np.repeat(np.exp2(scales.astype(np.float64) - 127.0), 8, axis=1)[..., None]
    return vals.transpose(0, 1, 3, 2).reshape(g * 512, n)


K, L, T, B, N = 512, 1024, 1024, 512, 512


def setup_inputs():
    n = np.random.standard_normal
    fk = mx_kscale(K)
    fl = mx_kscale(L)
    wap = pack_weight(n((K, N)) * 1 / np.sqrt(K) * fk[:, None], "e2m1")
    wbp = pack_weight(n((K, N)) * 1 / np.sqrt(K) * fk[:, None], "e4m3")
    xqp = pack_weight(n((L, B)) / fl[:, None], "e2m1")
    wqp = pack_weight(n((L, N)) * 1 / np.sqrt(L) * fl[:, None], "e4m3")
    return {
        "xf": (n((K, T))).astype(np.float32),
        "fa": (np.random.uniform(0.5, 2.0, (K, 1)) / fk[:, None]).astype(np.float32),
        "fb": (np.random.uniform(0.5, 2.0, (K, 1)) / fk[:, None]).astype(np.float32),
        "wa_words": wap[0],
        "wa_scales": wap[1],
        "wb_words": wbp[0],
        "wb_scales": wbp[1],
        "xq_words": xqp[0],
        "xq_scales": xqp[1],
        "wq_words": wqp[0],
        "wq_scales": wqp[1],
    }


def reference(xf, fa, fb, wa_words, wa_scales, wb_words, wb_scales, xq_words, xq_scales, wq_words, wq_scales):
    wau = unpack_weight(wa_words, wa_scales, "e2m1")
    wbu = unpack_weight(wb_words, wb_scales, "e4m3")
    xqu = unpack_weight(xq_words, xq_scales, "e2m1")
    wqu = unpack_weight(wq_words, wq_scales, "e4m3")
    u = f64(xf).reshape(K, B, T // B).max(axis=2) * f64(fa)
    v = 0.3 * np.square(f64(xf).reshape(K, B, T // B).sum(axis=2)) * f64(fb)
    uq = mxq(u, 0, "e4m3")
    vq = mxq(v, 0, "e5m2")
    y = wau.T @ uq + wbu.T @ vq + wqu.T @ xqu
    return y

@@ -1,0 +1,219 @@
+from contextlib import ExitStack
+
+import concourse.mybir as mybir
+
+K, L, T, B, N = 512, 1024, 1024, 512, 512
+FLOPS = 2 * N * B * (K + K + L)
+
+F32 = mybir.dt.float32
+BF16 = mybir.dt.bfloat16
+I32 = mybir.dt.int32
+U32 = mybir.dt.uint32
+U8 = mybir.dt.uint8
+E4M3 = mybir.dt.float8_e4m3fn_x4
+E5M2 = mybir.dt.float8_e5m2_x4
+E2M1 = mybir.dt.float4_e2m1fn_x4
+ALU = mybir.AluOpType
+ACT = mybir.ActivationFunctionType
+
+P = 128
+PACK = 4
+CB = 128
+CHUNKS = B // CB
+NT = N // P
+ZL = L // (P * PACK)
+
+
+def tile_mix_features_pooled_over_tokens_kernel(
+    tc, xf, fa, fb, wa_words, wa_scales, wb_words, wb_scales, xq_words, xq_scales, wq_words, wq_scales, out
+):
+    nc = tc.nc
+    with ExitStack() as ctx:
+        sb = ctx.enter_context(tc.tile_pool(name="sb", bufs=1))
+        ps = ctx.enter_context(tc.psum_pool(name="ps", bufs=1))
+        ctx.enter_context(tc.manual_schedule())
+
+        def tiles(name, count, shape, dtype):
+            return [sb.tile(shape, dtype, name="%s%d" % (name, i), align_bytes=64) for i in range(count)]
+
+        x_first = tiles("x_first", 2, [P, 2, 2 * CB], F32)
+        x_rest = tiles("x_rest", CHUNKS - 1, [P, PACK, 2 * CB], F32)
+        fa_t = sb.tile([P, PACK], F32, name="fa_t")
+        fb_t = sb.tile([P, PACK], F32, name="fb_t")
+        sums = tiles("sums", CHUNKS, [P, PACK, CB], F32)
+        maxes = tiles("maxes", CHUNKS, [P, PACK, CB], F32)
+        squares = tiles("squares", CHUNKS, [P, CB, PACK], F32)
+        u_rows = tiles("u_rows", CHUNKS, [P, PACK, CB], BF16)
+        u_in = tiles("u_in", CHUNKS, [P, CB, PACK], BF16)
+        v_in = tiles("v_in", CHUNKS, [P, CB, PACK], BF16)
+        u_codes = tiles("u_codes", CHUNKS, [P, CB], U32)
+        u_plane = tiles("u_plane", CHUNKS, [P, CB], U8)
+        v_codes = sb.tile([P, B], U32, name="v_codes", align_bytes=64)
+        v_plane = sb.tile([P, B], U8, name="v_plane", align_bytes=64)
+        wa_t = sb.tile([P, 2 * N], U8, name="wa_t", align_bytes=64)
+        wb_t = sb.tile([P, N], U32, name="wb_t", align_bytes=64)
+        wq_t = tiles("wq_t", ZL, [P, N], U32)
+        xq_t = sb.tile([P, ZL, 2 * B], U8, name="xq_t", align_bytes=64)
+        wa_plane = sb.tile([P, 1, N], U8, name="wa_plane", align_bytes=64)
+        wb_plane = sb.tile([P, 1, N], U8, name="wb_plane", align_bytes=64)
+        wq_plane = sb.tile([P, ZL, N], U8, name="wq_plane", align_bytes=64)
+        xq_plane = sb.tile([P, ZL, B], U8, name="xq_plane", align_bytes=64)
+        result = tiles("result", NT, [P, B], F32)
+        acc = [ps.tile([P, B], F32, name="acc%d" % i) for i in range(NT)]
+
+        x_rows = xf.rearrange("(p j) t -> p j t", j=PACK)
+
+        def load_x(c):
+            nc.sync.dma_start(out=x_rest[c - 1][:], in_=x_rows[:, :, 2 * CB * c : 2 * CB * (c + 1)])
+
+        def load_scale_rows(plane, scales, r):
+            src = scales.rearrange("z (q r) n -> r q z n", r=4)[r]
+            nc.sync.dma_start(out=plane[r:P:32].bitcast(I32), in_=src.bitcast(I32))
+
+        def load_words8(tile, words, z):
+            nc.sync.dma_start(out=tile[:].bitcast(I32), in_=words[z].rearrange("p n t -> p (n t)").bitcast(I32))
+
+        for plane in (xq_plane, wq_plane, wb_plane, wa_plane):
+            nc.vector.memset(plane[:].bitcast(I32), 0)
+
+        nc.scalar.dma_start(out=fa_t[:], in_=fa.rearrange("(p j) o -> p (j o)", j=PACK))
+        nc.scalar.dma_start(out=fb_t[:], in_=fb.rearrange("(p j) o -> p (j o)", j=PACK))
+        for h in range(2):
+            nc.sync.dma_start(out=x_first[h][:], in_=x_rows[:, 2 * h : 2 * h + 2, 0 : 2 * CB])
+        load_x(1)
+        for r in range(4):
+            load_scale_rows(xq_plane, xq_scales, r)
+        load_scale_rows(wq_plane, wq_scales, 0)
+        nc.sync.dma_start(out=xq_t[:].bitcast(I32), in_=xq_words.rearrange("z p c -> p z c").bitcast(I32))
+        load_scale_rows(wq_plane, wq_scales, 1)
+        load_words8(wq_t[0], wq_words, 0)
+        load_scale_rows(wq_plane, wq_scales, 2)
+        load_scale_rows(wq_plane, wq_scales, 3)
+        load_x(2)
+        load_words8(wq_t[1], wq_words, 1)
+        load_x(3)
+        nc.sync.dma_start(out=wa_t[:].bitcast(I32), in_=wa_words[0].bitcast(I32))
+        for r in range(4):
+            load_scale_rows(wa_plane, wa_scales, r)
+        load_words8(wb_t, wb_words, 0)
+        for r in range(4):
+            load_scale_rows(wb_plane, wb_scales, r)
+
+        def pool_pairs(dst, c, op):
+            if c == 0:
+                for h in range(2):
+                    src = x_first[h]
+                    nc.vector.tensor_tensor(
+                        out=dst[0][:, 2 * h : 2 * h + 2, :], in0=src[:, :, 0::2], in1=src[:, :, 1::2], op=op
+                    )
+            else:
+                src = x_rest[c - 1]
+                nc.vector.tensor_tensor(out=dst[c][:], in0=src[:, :, 0::2], in1=src[:, :, 1::2], op=op)
+
+        def square(c):
+            nc.scalar.activation(
+                out=squares[c][:].rearrange("p (g i) j -> p g j i", i=2),
+                in_=sums[c][:].rearrange("p j (g i) -> p g j i", i=2),
+                func=ACT.Square,
+            )
+
+        def scale_u(c):
+            for j in range(PACK):
+                nc.scalar.activation(
+                    out=u_rows[c][:, j, :], in_=maxes[c][:, j, :], func=ACT.Copy, scale=fa_t[:, j : j + 1]
+                )
+
+        def interleave_u(c):
+            nc.scalar.copy(
+                out=u_in[c][:].rearrange("p (g i) j -> p g j i", i=4),
+                in_=u_rows[c][:].rearrange("p j (g i) -> p g j i", i=4),
+            )
+
+        def scale_v(c):
+            nc.vector.scalar_tensor_tensor(
+                out=v_in[c][:],
+                in0=squares[c][:],
+                scalar=0.3,
+                in1=fb_t[:].unsqueeze(1).to_broadcast([P, CB, PACK]),
+                op0=ALU.mult,
+                op1=ALU.mult,
+            )
+
+        def quantize_u(c):
+            nc.vector.quantize_mx(
+                out=u_codes[c][:].bitcast(E4M3), scales=u_plane[c][:], in_=u_in[c][:].rearrange("p b j -> p (b j)")
+            )
+
+        def quantize_v(c):
+            cols = slice(c * CB, (c + 1) * CB)
+            nc.vector.quantize_mx(
+                out=v_codes[:, cols].bitcast(E5M2), scales=v_plane[:, cols], in_=v_in[c][:].rearrange("p b j -> p (b j)")
+            )
+
+        def pass_q(n, z):
+            cols = slice(n * P, (n + 1) * P)
+            nc.tensor.matmul_mx(
+                out=acc[n][:],
+                lhsT=wq_t[z][:, cols].bitcast(E4M3),
+                lhsT_scale=wq_plane[:, z, cols],
+                rhs=xq_t[:, z, :].bitcast(E2M1),
+                rhs_scale=xq_plane[:, z, :],
+                start=(z == 0),
+                stop=False,
+            )
+
+        def pass_u(n, c):
+            nc.tensor.matmul_mx(
+                out=acc[n][:, c * CB : (c + 1) * CB],
+                lhsT=wa_t[:, 2 * n * P : 2 * (n + 1) * P].bitcast(E2M1),
+                lhsT_scale=wa_plane[:, 0, n * P : (n + 1) * P],
+                rhs=u_codes[c][:].bitcast(E4M3),
+                rhs_scale=u_plane[c][:],
+                start=False,
+                stop=(c == CHUNKS - 1),
+            )
+
+        def pass_v(n):
+            cols = slice(n * P, (n + 1) * P)
+            nc.tensor.matmul_mx(
+                out=acc[n][:],
+                lhsT=wb_t[:, cols].bitcast(E4M3),
+                lhsT_scale=wb_plane[:, 0, cols],
+                rhs=v_codes[:].bitcast(E5M2),
+                rhs_scale=v_plane[:],
+                start=False,
+                stop=False,
+            )
+
+        pool_pairs(sums, 0, ALU.add)
+        pool_pairs(maxes, 0, ALU.max)
+        square(0)
+        scale_u(0)
+        interleave_u(0)
+        for c in range(1, CHUNKS):
+            pool_pairs(sums, c, ALU.add)
+            scale_v(c - 1)
+            pool_pairs(maxes, c, ALU.max)
+            square(c)
+            scale_u(c)
+            interleave_u(c)
+            quantize_v(c - 1)
+            quantize_u(c - 1)
+        scale_v(CHUNKS - 1)
+        quantize_v(CHUNKS - 1)
+        quantize_u(CHUNKS - 1)
+
+        for z in range(ZL):
+            for n in range(NT):
+                pass_q(n, z)
+        for c in range(CHUNKS - 1):
+            for n in range(NT):
+                pass_u(n, c)
+        for n in range(NT):
+            pass_v(n)
+            pass_u(n, CHUNKS - 1)
+            if n % 2 == 0:
+                nc.scalar.copy(out=result[n][:], in_=acc[n][:])
+            else:
+                nc.vector.tensor_copy(out=result[n][:], in_=acc[n][:])
+            nc.sync.dma_start(out=out[n * P : (n + 1) * P, :], in_=result[n][:])

@@ -18,8 +18,10 @@ ACT = mybir.ActivationFunctionType
 
 P = 128
 PACK = 4
-CB = 128
-CHUNKS = B // CB
+WIDTHS = (64, 128, 128, 128, 64)
+STARTS = tuple(sum(WIDTHS[:c]) for c in range(len(WIDTHS)))
+CHUNKS = len(WIDTHS)
+LAST = CHUNKS - 1
 NT = N // P
 ZL = L // (P * PACK)
 
@@ -36,18 +38,20 @@ def tile_mix_features_pooled_over_tokens_kernel(
         def tiles(name, count, shape, dtype):
             return [sb.tile(shape, dtype, name="%s%d" % (name, i), align_bytes=64) for i in range(count)]
 
-        x_first = tiles("x_first", 2, [P, 2, 2 * CB], F32)
-        x_rest = tiles("x_rest", CHUNKS - 1, [P, PACK, 2 * CB], F32)
+        def chunk_tiles(name, shape_of, dtype, count=CHUNKS):
+            return [sb.tile(shape_of(WIDTHS[c]), dtype, name="%s%d" % (name, c), align_bytes=64) for c in range(count)]
+
+        x_t = chunk_tiles("x_t", lambda w: [P, PACK, 2 * w], F32)
         fa_t = sb.tile([P, PACK], F32, name="fa_t")
         fb_t = sb.tile([P, PACK], F32, name="fb_t")
-        sums = tiles("sums", CHUNKS, [P, PACK, CB], F32)
-        maxes = tiles("maxes", CHUNKS, [P, PACK, CB], F32)
-        squares = tiles("squares", CHUNKS, [P, CB, PACK], F32)
-        u_rows = tiles("u_rows", CHUNKS, [P, PACK, CB], BF16)
-        u_in = tiles("u_in", CHUNKS, [P, CB, PACK], BF16)
-        v_in = tiles("v_in", CHUNKS, [P, CB, PACK], BF16)
-        u_codes = tiles("u_codes", CHUNKS, [P, CB], U32)
-        u_plane = tiles("u_plane", CHUNKS, [P, CB], U8)
+        sums = chunk_tiles("sums", lambda w: [P, PACK, w], F32)
+        maxes = chunk_tiles("maxes", lambda w: [P, PACK, w], F32)
+        squares = chunk_tiles("squares", lambda w: [P, w, PACK], F32)
+        u_rows = chunk_tiles("u_rows", lambda w: [P, PACK, w], BF16, LAST)
+        u_in = chunk_tiles("u_in", lambda w: [P, w, PACK], BF16)
+        v_in = chunk_tiles("v_in", lambda w: [P, w, PACK], BF16)
+        u_codes = sb.tile([P, B], U32, name="u_codes", align_bytes=64)
+        u_plane = sb.tile([P, B], U8, name="u_plane", align_bytes=64)
         v_codes = sb.tile([P, B], U32, name="v_codes", align_bytes=64)
         v_plane = sb.tile([P, B], U8, name="v_plane", align_bytes=64)
         wa_t = sb.tile([P, 2 * N], U8, name="wa_t", align_bytes=64)
@@ -64,7 +68,7 @@ def tile_mix_features_pooled_over_tokens_kernel(
         x_rows = xf.rearrange("(p j) t -> p j t", j=PACK)
 
         def load_x(c):
-            nc.sync.dma_start(out=x_rest[c - 1][:], in_=x_rows[:, :, 2 * CB * c : 2 * CB * (c + 1)])
+            nc.sync.dma_start(out=x_t[c][:], in_=x_rows[:, :, 2 * STARTS[c] : 2 * (STARTS[c] + WIDTHS[c])])
 
         def load_scale_rows(plane, scales, r):
             src = scales.rearrange("z (q r) n -> r q z n", r=4)[r]
@@ -78,37 +82,40 @@ def tile_mix_features_pooled_over_tokens_kernel(
 
         nc.scalar.dma_start(out=fa_t[:], in_=fa.rearrange("(p j) o -> p (j o)", j=PACK))
         nc.scalar.dma_start(out=fb_t[:], in_=fb.rearrange("(p j) o -> p (j o)", j=PACK))
-        for h in range(2):
-            nc.sync.dma_start(out=x_first[h][:], in_=x_rows[:, 2 * h : 2 * h + 2, 0 : 2 * CB])
-        load_x(1)
+        for c in range(3):
+            load_x(c)
         for r in range(4):
             load_scale_rows(xq_plane, xq_scales, r)
-        load_scale_rows(wq_plane, wq_scales, 0)
         nc.sync.dma_start(out=xq_t[:].bitcast(I32), in_=xq_words.rearrange("z p c -> p z c").bitcast(I32))
-        load_scale_rows(wq_plane, wq_scales, 1)
-        load_words8(wq_t[0], wq_words, 0)
-        load_scale_rows(wq_plane, wq_scales, 2)
-        load_scale_rows(wq_plane, wq_scales, 3)
-        load_x(2)
-        load_words8(wq_t[1], wq_words, 1)
         load_x(3)
-        nc.sync.dma_start(out=wa_t[:].bitcast(I32), in_=wa_words[0].bitcast(I32))
-        for r in range(4):
-            load_scale_rows(wa_plane, wa_scales, r)
-        load_words8(wb_t, wb_words, 0)
-        for r in range(4):
+        for r in (0, 1):
+            load_scale_rows(wq_plane, wq_scales, r)
+        load_words8(wq_t[0], wq_words, 0)
+        for r in (2, 3):
+            load_scale_rows(wq_plane, wq_scales, r)
+        load_x(4)
+        for r in (0, 1):
             load_scale_rows(wb_plane, wb_scales, r)
+        load_words8(wq_t[1], wq_words, 1)
+        for r in (2, 3):
+            load_scale_rows(wb_plane, wb_scales, r)
+        load_words8(wb_t, wb_words, 0)
+        for r in (0, 1):
+            load_scale_rows(wa_plane, wa_scales, r)
+        nc.sync.dma_start(out=wa_t[:].bitcast(I32), in_=wa_words[0].bitcast(I32))
+        for r in (2, 3):
+            load_scale_rows(wa_plane, wa_scales, r)
 
         def pool_pairs(dst, c, op):
-            if c == 0:
-                for h in range(2):
-                    src = x_first[h]
-                    nc.vector.tensor_tensor(
-                        out=dst[0][:, 2 * h : 2 * h + 2, :], in0=src[:, :, 0::2], in1=src[:, :, 1::2], op=op
-                    )
-            else:
-                src = x_rest[c - 1]
-                nc.vector.tensor_tensor(out=dst[c][:], in0=src[:, :, 0::2], in1=src[:, :, 1::2], op=op)
+            nc.vector.tensor_tensor(out=dst[c][:], in0=x_t[c][:, :, 0::2], in1=x_t[c][:, :, 1::2], op=op)
+
+        def scale_interleave_u(c):
+            nc.vector.tensor_tensor(
+                out=u_in[c][:].rearrange("p (g i) j -> p g j i", i=2),
+                in0=maxes[c][:].rearrange("p j (g i) -> p g j i", i=2),
+                in1=fa_t[:].unsqueeze(1).unsqueeze(3).to_broadcast([P, WIDTHS[c] // 2, PACK, 2]),
+                op=ALU.mult,
+            )
 
         def square(c):
             nc.scalar.activation(
@@ -134,18 +141,19 @@ def tile_mix_features_pooled_over_tokens_kernel(
                 out=v_in[c][:],
                 in0=squares[c][:],
                 scalar=0.3,
-                in1=fb_t[:].unsqueeze(1).to_broadcast([P, CB, PACK]),
+                in1=fb_t[:].unsqueeze(1).to_broadcast([P, WIDTHS[c], PACK]),
                 op0=ALU.mult,
                 op1=ALU.mult,
             )
 
         def quantize_u(c):
+            cols = slice(STARTS[c], STARTS[c] + WIDTHS[c])
             nc.vector.quantize_mx(
-                out=u_codes[c][:].bitcast(E4M3), scales=u_plane[c][:], in_=u_in[c][:].rearrange("p b j -> p (b j)")
+                out=u_codes[:, cols].bitcast(E4M3), scales=u_plane[:, cols], in_=u_in[c][:].rearrange("p b j -> p (b j)")
             )
 
         def quantize_v(c):
-            cols = slice(c * CB, (c + 1) * CB)
+            cols = slice(STARTS[c], STARTS[c] + WIDTHS[c])
             nc.vector.quantize_mx(
                 out=v_codes[:, cols].bitcast(E5M2), scales=v_plane[:, cols], in_=v_in[c][:].rearrange("p b j -> p (b j)")
             )
@@ -162,15 +170,15 @@ def tile_mix_features_pooled_over_tokens_kernel(
                 stop=False,
             )
 
-        def pass_u(n, c):
+        def pass_u(n):
             nc.tensor.matmul_mx(
-                out=acc[n][:, c * CB : (c + 1) * CB],
+                out=acc[n][:],
                 lhsT=wa_t[:, 2 * n * P : 2 * (n + 1) * P].bitcast(E2M1),
                 lhsT_scale=wa_plane[:, 0, n * P : (n + 1) * P],
-                rhs=u_codes[c][:].bitcast(E4M3),
-                rhs_scale=u_plane[c][:],
+                rhs=u_codes[:].bitcast(E4M3),
+                rhs_scale=u_plane[:],
                 start=False,
-                stop=(c == CHUNKS - 1),
+                stop=True,
             )
 
         def pass_v(n):
@@ -189,31 +197,44 @@ def tile_mix_features_pooled_over_tokens_kernel(
         pool_pairs(maxes, 0, ALU.max)
         square(0)
         scale_u(0)
-        interleave_u(0)
-        for c in range(1, CHUNKS):
+        for c in range(1, LAST):
             pool_pairs(sums, c, ALU.add)
+            if c > 1:
+                quantize_u(c - 2)
             scale_v(c - 1)
             pool_pairs(maxes, c, ALU.max)
-            square(c)
-            scale_u(c)
-            interleave_u(c)
             quantize_v(c - 1)
-            quantize_u(c - 1)
-        scale_v(CHUNKS - 1)
-        quantize_v(CHUNKS - 1)
-        quantize_u(CHUNKS - 1)
+            square(c)
+            interleave_u(c - 1)
+            scale_u(c)
+        pool_pairs(sums, LAST, ALU.add)
+        pool_pairs(maxes, LAST, ALU.max)
+        square(LAST)
+        interleave_u(LAST - 1)
+        quantize_u(LAST - 2)
+        scale_v(LAST - 1)
+        scale_interleave_u(LAST)
+        scale_v(LAST)
+        quantize_v(LAST - 1)
+        quantize_u(LAST)
+        quantize_v(LAST)
+        quantize_u(LAST - 1)
 
         for z in range(ZL):
             for n in range(NT):
                 pass_q(n, z)
-        for c in range(CHUNKS - 1):
-            for n in range(NT):
-                pass_u(n, c)
         for n in range(NT):
             pass_v(n)
-            pass_u(n, CHUNKS - 1)
-            if n % 2 == 0:
+            pass_u(n)
+            rows = slice(n * P, (n + 1) * P)
+            if n == 0:
+                for h in range(2):
+                    half = slice(h * B // 2, (h + 1) * B // 2)
+                    nc.scalar.copy(out=result[n][:, half], in_=acc[n][:, half])
+                    nc.sync.dma_start(out=out[rows, half], in_=result[n][:, half])
+            elif n % 2 == 0:
                 nc.scalar.copy(out=result[n][:], in_=acc[n][:])
+                nc.scalar.dma_start(out=out[rows, :], in_=result[n][:])
             else:
                 nc.vector.tensor_copy(out=result[n][:], in_=acc[n][:])
-            nc.sync.dma_start(out=out[n * P : (n + 1) * P, :], in_=result[n][:])
+                nc.sync.dma_start(out=out[rows, :], in_=result[n][:])

@@ -18,7 +18,8 @@ ACT = mybir.ActivationFunctionType
 
 P = 128
 PACK = 4
-WIDTHS = (64, 128, 128, 128, 64)
+WIDTHS = (32, 64, 96, 128, 128, 64)
+QW = 128
 STARTS = tuple(sum(WIDTHS[:c]) for c in range(len(WIDTHS)))
 CHUNKS = len(WIDTHS)
 LAST = CHUNKS - 1
@@ -48,8 +49,8 @@ def tile_mix_features_pooled_over_tokens_kernel(
         maxes = chunk_tiles("maxes", lambda w: [P, PACK, w], F32)
         squares = chunk_tiles("squares", lambda w: [P, w, PACK], F32)
         u_rows = chunk_tiles("u_rows", lambda w: [P, PACK, w], BF16, LAST)
-        u_in = chunk_tiles("u_in", lambda w: [P, w, PACK], BF16)
-        v_in = chunk_tiles("v_in", lambda w: [P, w, PACK], BF16)
+        u_in = sb.tile([P, B * PACK], BF16, name="u_in", align_bytes=64)
+        v_in = sb.tile([P, B * PACK], BF16, name="v_in", align_bytes=64)
         u_codes = sb.tile([P, B], U32, name="u_codes", align_bytes=64)
         u_plane = sb.tile([P, B], U8, name="u_plane", align_bytes=64)
         v_codes = sb.tile([P, B], U32, name="v_codes", align_bytes=64)
@@ -70,48 +71,46 @@ def tile_mix_features_pooled_over_tokens_kernel(
         def load_x(c):
             nc.sync.dma_start(out=x_t[c][:], in_=x_rows[:, :, 2 * STARTS[c] : 2 * (STARTS[c] + WIDTHS[c])])
 
-        def load_scale_rows(plane, scales, r):
+        def chunk_of(tile, c):
+            return tile[:, PACK * STARTS[c] : PACK * (STARTS[c] + WIDTHS[c])]
+
+        def load_scale_rows(queue, plane, scales, r):
             src = scales.rearrange("z (q r) n -> r q z n", r=4)[r]
-            nc.sync.dma_start(out=plane[r:P:32].bitcast(I32), in_=src.bitcast(I32))
+            queue.dma_start(out=plane[r:P:32].bitcast(I32), in_=src.bitcast(I32))
 
         def load_words8(tile, words, z):
             nc.sync.dma_start(out=tile[:].bitcast(I32), in_=words[z].rearrange("p n t -> p (n t)").bitcast(I32))
 
-        for plane in (xq_plane, wq_plane, wb_plane, wa_plane):
+        for plane in (xq_plane, wa_plane):
             nc.vector.memset(plane[:].bitcast(I32), 0)
+        for plane in (wq_plane, wb_plane):
+            nc.gpsimd.memset(plane[:].bitcast(I32), 0)
+        for plane, scales in ((wq_plane, wq_scales), (wb_plane, wb_scales)):
+            for r in range(4):
+                load_scale_rows(nc.gpsimd, plane, scales, r)
 
         nc.scalar.dma_start(out=fa_t[:], in_=fa.rearrange("(p j) o -> p (j o)", j=PACK))
         nc.scalar.dma_start(out=fb_t[:], in_=fb.rearrange("(p j) o -> p (j o)", j=PACK))
-        for c in range(3):
+        for c in range(4):
             load_x(c)
         for r in range(4):
-            load_scale_rows(xq_plane, xq_scales, r)
-        nc.sync.dma_start(out=xq_t[:].bitcast(I32), in_=xq_words.rearrange("z p c -> p z c").bitcast(I32))
-        load_x(3)
-        for r in (0, 1):
-            load_scale_rows(wq_plane, wq_scales, r)
-        load_words8(wq_t[0], wq_words, 0)
-        for r in (2, 3):
-            load_scale_rows(wq_plane, wq_scales, r)
+            load_scale_rows(nc.sync, xq_plane, xq_scales, r)
         load_x(4)
-        for r in (0, 1):
-            load_scale_rows(wb_plane, wb_scales, r)
+        nc.sync.dma_start(out=xq_t[:].bitcast(I32), in_=xq_words.rearrange("z p c -> p z c").bitcast(I32))
+        load_words8(wq_t[0], wq_words, 0)
+        load_x(5)
         load_words8(wq_t[1], wq_words, 1)
-        for r in (2, 3):
-            load_scale_rows(wb_plane, wb_scales, r)
+        for r in range(4):
+            load_scale_rows(nc.sync, wa_plane, wa_scales, r)
         load_words8(wb_t, wb_words, 0)
-        for r in (0, 1):
-            load_scale_rows(wa_plane, wa_scales, r)
         nc.sync.dma_start(out=wa_t[:].bitcast(I32), in_=wa_words[0].bitcast(I32))
-        for r in (2, 3):
-            load_scale_rows(wa_plane, wa_scales, r)
 
         def pool_pairs(dst, c, op):
             nc.vector.tensor_tensor(out=dst[c][:], in0=x_t[c][:, :, 0::2], in1=x_t[c][:, :, 1::2], op=op)
 
         def scale_interleave_u(c):
             nc.vector.tensor_tensor(
-                out=u_in[c][:].rearrange("p (g i) j -> p g j i", i=2),
+                out=chunk_of(u_in, c).rearrange("p (g i j) -> p g j i", i=2, j=PACK),
                 in0=maxes[c][:].rearrange("p j (g i) -> p g j i", i=2),
                 in1=fa_t[:].unsqueeze(1).unsqueeze(3).to_broadcast([P, WIDTHS[c] // 2, PACK, 2]),
                 op=ALU.mult,
@@ -132,13 +131,13 @@ def tile_mix_features_pooled_over_tokens_kernel(
 
         def interleave_u(c):
             nc.scalar.copy(
-                out=u_in[c][:].rearrange("p (g i) j -> p g j i", i=4),
+                out=chunk_of(u_in, c).rearrange("p (g i j) -> p g j i", i=4, j=PACK),
                 in_=u_rows[c][:].rearrange("p j (g i) -> p g j i", i=4),
             )
 
         def scale_v(c):
             nc.vector.scalar_tensor_tensor(
-                out=v_in[c][:],
+                out=chunk_of(v_in, c).rearrange("p (b j) -> p b j", j=PACK),
                 in0=squares[c][:],
                 scalar=0.3,
                 in1=fb_t[:].unsqueeze(1).to_broadcast([P, WIDTHS[c], PACK]),
@@ -146,17 +145,20 @@ def tile_mix_features_pooled_over_tokens_kernel(
                 op1=ALU.mult,
             )
 
-        def quantize_u(c):
-            cols = slice(STARTS[c], STARTS[c] + WIDTHS[c])
+        def quantize(src, codes, plane, fmt, w):
+            cols = slice(w * QW, (w + 1) * QW)
             nc.vector.quantize_mx(
-                out=u_codes[:, cols].bitcast(E4M3), scales=u_plane[:, cols], in_=u_in[c][:].rearrange("p b j -> p (b j)")
+                out=codes[:, cols].bitcast(fmt), scales=plane[:, cols], in_=src[:, PACK * QW * w : PACK * QW * (w + 1)]
             )
 
-        def quantize_v(c):
-            cols = slice(STARTS[c], STARTS[c] + WIDTHS[c])
-            nc.vector.quantize_mx(
-                out=v_codes[:, cols].bitcast(E5M2), scales=v_plane[:, cols], in_=v_in[c][:].rearrange("p b j -> p (b j)")
-            )
+        def quantize_u(w):
+            quantize(u_in, u_codes, u_plane, E4M3, w)
+
+        def quantize_v(w):
+            quantize(v_in, v_codes, v_plane, E5M2, w)
+
+        def windows_closed_by(c):
+            return range(STARTS[c] // QW, (STARTS[c] + WIDTHS[c]) // QW)
 
         def pass_q(n, z):
             cols = slice(n * P, (n + 1) * P)
@@ -200,10 +202,12 @@ def tile_mix_features_pooled_over_tokens_kernel(
         for c in range(1, LAST):
             pool_pairs(sums, c, ALU.add)
             if c > 1:
-                quantize_u(c - 2)
+                for w in windows_closed_by(c - 2):
+                    quantize_u(w)
             scale_v(c - 1)
             pool_pairs(maxes, c, ALU.max)
-            quantize_v(c - 1)
+            for w in windows_closed_by(c - 1):
+                quantize_v(w)
             square(c)
             interleave_u(c - 1)
             scale_u(c)
@@ -211,14 +215,15 @@ def tile_mix_features_pooled_over_tokens_kernel(
         pool_pairs(maxes, LAST, ALU.max)
         square(LAST)
         interleave_u(LAST - 1)
-        quantize_u(LAST - 2)
+        for w in windows_closed_by(LAST - 2):
+            quantize_u(w)
         scale_v(LAST - 1)
         scale_interleave_u(LAST)
         scale_v(LAST)
-        quantize_v(LAST - 1)
-        quantize_u(LAST)
-        quantize_v(LAST)
-        quantize_u(LAST - 1)
+        for c in (LAST - 1, LAST):
+            for w in windows_closed_by(c):
+                quantize_v(w)
+                quantize_u(w)
 
         for z in range(ZL):
             for n in range(NT):

@@ -18,7 +18,7 @@ ACT = mybir.ActivationFunctionType
 
 P = 128
 PACK = 4
-WIDTHS = (32, 64, 96, 128, 128, 64)
+WIDTHS = (64, 96, 128, 144, 80)
 QW = 128
 STARTS = tuple(sum(WIDTHS[:c]) for c in range(len(WIDTHS)))
 CHUNKS = len(WIDTHS)
@@ -81,29 +81,35 @@ def tile_mix_features_pooled_over_tokens_kernel(
         def load_words8(tile, words, z):
             nc.sync.dma_start(out=tile[:].bitcast(I32), in_=words[z].rearrange("p n t -> p (n t)").bitcast(I32))
 
-        for plane in (xq_plane, wa_plane):
+        for plane in (xq_plane, wq_plane, wb_plane, wa_plane):
             nc.vector.memset(plane[:].bitcast(I32), 0)
-        for plane in (wq_plane, wb_plane):
-            nc.gpsimd.memset(plane[:].bitcast(I32), 0)
-        for plane, scales in ((wq_plane, wq_scales), (wb_plane, wb_scales)):
-            for r in range(4):
-                load_scale_rows(nc.gpsimd, plane, scales, r)
+        for plane, scales in ((xq_plane, xq_scales), (wq_plane, wq_scales), (wb_plane, wb_scales), (wa_plane, wa_scales)):
+            load_scale_rows(nc.gpsimd, plane, scales, 3)
 
         nc.scalar.dma_start(out=fa_t[:], in_=fa.rearrange("(p j) o -> p (j o)", j=PACK))
         nc.scalar.dma_start(out=fb_t[:], in_=fb.rearrange("(p j) o -> p (j o)", j=PACK))
-        for c in range(4):
-            load_x(c)
-        for r in range(4):
-            load_scale_rows(nc.sync, xq_plane, xq_scales, r)
-        load_x(4)
+        load_x(0)
+        load_x(1)
+        load_scale_rows(nc.sync, xq_plane, xq_scales, 0)
+        load_scale_rows(nc.sync, xq_plane, xq_scales, 1)
+        load_scale_rows(nc.sync, xq_plane, xq_scales, 2)
+        load_x(2)
+        load_x(3)
         nc.sync.dma_start(out=xq_t[:].bitcast(I32), in_=xq_words.rearrange("z p c -> p z c").bitcast(I32))
+        load_scale_rows(nc.sync, wq_plane, wq_scales, 0)
         load_words8(wq_t[0], wq_words, 0)
-        load_x(5)
+        load_scale_rows(nc.sync, wq_plane, wq_scales, 1)
+        load_scale_rows(nc.sync, wq_plane, wq_scales, 2)
+        load_x(4)
         load_words8(wq_t[1], wq_words, 1)
-        for r in range(4):
-            load_scale_rows(nc.sync, wa_plane, wa_scales, r)
         load_words8(wb_t, wb_words, 0)
         nc.sync.dma_start(out=wa_t[:].bitcast(I32), in_=wa_words[0].bitcast(I32))
+        load_scale_rows(nc.sync, wb_plane, wb_scales, 0)
+        load_scale_rows(nc.sync, wb_plane, wb_scales, 1)
+        load_scale_rows(nc.sync, wb_plane, wb_scales, 2)
+        load_scale_rows(nc.sync, wa_plane, wa_scales, 0)
+        load_scale_rows(nc.sync, wa_plane, wa_scales, 1)
+        load_scale_rows(nc.sync, wa_plane, wa_scales, 2)
 
         def pool_pairs(dst, c, op):
             nc.vector.tensor_tensor(out=dst[c][:], in0=x_t[c][:, :, 0::2], in1=x_t[c][:, :, 1::2], op=op)

@@ -2,7 +2,7 @@ from contextlib import ExitStack
 
 import concourse.mybir as mybir
 
-K, L, T, B, N = 512, 1024, 1024, 512, 512
+K, L, B, N = 512, 1024, 512, 512
 FLOPS = 2 * N * B * (K + K + L)
 
 F32 = mybir.dt.float32
@@ -18,13 +18,14 @@ ACT = mybir.ActivationFunctionType
 
 P = 128
 PACK = 4
+ROWS_PER_QUADRANT = 4
+N_TILES = N // P
+L_PASSES = L // (P * PACK)
+
 WIDTHS = (64, 96, 128, 144, 80)
-QW = 128
 STARTS = tuple(sum(WIDTHS[:c]) for c in range(len(WIDTHS)))
-CHUNKS = len(WIDTHS)
-LAST = CHUNKS - 1
-NT = N // P
-ZL = L // (P * PACK)
+LAST = len(WIDTHS) - 1
+WINDOW = 128
 
 
 def tile_mix_features_pooled_over_tokens_kernel(
@@ -36,19 +37,16 @@ def tile_mix_features_pooled_over_tokens_kernel(
         ps = ctx.enter_context(tc.psum_pool(name="ps", bufs=1))
         ctx.enter_context(tc.manual_schedule())
 
-        def tiles(name, count, shape, dtype):
-            return [sb.tile(shape, dtype, name="%s%d" % (name, i), align_bytes=64) for i in range(count)]
+        def tiles(name, shapes, dtype):
+            return [sb.tile(shape, dtype, name="%s%d" % (name, i), align_bytes=64) for i, shape in enumerate(shapes)]
 
-        def chunk_tiles(name, shape_of, dtype, count=CHUNKS):
-            return [sb.tile(shape_of(WIDTHS[c]), dtype, name="%s%d" % (name, c), align_bytes=64) for c in range(count)]
-
-        x_t = chunk_tiles("x_t", lambda w: [P, PACK, 2 * w], F32)
+        x_t = tiles("x_t", [[P, PACK, 2 * w] for w in WIDTHS], F32)
         fa_t = sb.tile([P, PACK], F32, name="fa_t")
         fb_t = sb.tile([P, PACK], F32, name="fb_t")
-        sums = chunk_tiles("sums", lambda w: [P, PACK, w], F32)
-        maxes = chunk_tiles("maxes", lambda w: [P, PACK, w], F32)
-        squares = chunk_tiles("squares", lambda w: [P, w, PACK], F32)
-        u_rows = chunk_tiles("u_rows", lambda w: [P, PACK, w], BF16, LAST)
+        sums = tiles("sums", [[P, PACK, w] for w in WIDTHS], F32)
+        maxes = tiles("maxes", [[P, PACK, w] for w in WIDTHS], F32)
+        squares = tiles("squares", [[P, w, PACK] for w in WIDTHS], F32)
+        u_rows = tiles("u_rows", [[P, PACK, w] for w in WIDTHS[:LAST]], BF16)
         u_in = sb.tile([P, B * PACK], BF16, name="u_in", align_bytes=64)
         v_in = sb.tile([P, B * PACK], BF16, name="v_in", align_bytes=64)
         u_codes = sb.tile([P, B], U32, name="u_codes", align_bytes=64)
@@ -57,70 +55,32 @@ def tile_mix_features_pooled_over_tokens_kernel(
         v_plane = sb.tile([P, B], U8, name="v_plane", align_bytes=64)
         wa_t = sb.tile([P, 2 * N], U8, name="wa_t", align_bytes=64)
         wb_t = sb.tile([P, N], U32, name="wb_t", align_bytes=64)
-        wq_t = tiles("wq_t", ZL, [P, N], U32)
-        xq_t = sb.tile([P, ZL, 2 * B], U8, name="xq_t", align_bytes=64)
+        wq_t = tiles("wq_t", [[P, N]] * L_PASSES, U32)
+        xq_t = sb.tile([P, L_PASSES, 2 * B], U8, name="xq_t", align_bytes=64)
         wa_plane = sb.tile([P, 1, N], U8, name="wa_plane", align_bytes=64)
         wb_plane = sb.tile([P, 1, N], U8, name="wb_plane", align_bytes=64)
-        wq_plane = sb.tile([P, ZL, N], U8, name="wq_plane", align_bytes=64)
-        xq_plane = sb.tile([P, ZL, B], U8, name="xq_plane", align_bytes=64)
-        result = tiles("result", NT, [P, B], F32)
-        acc = [ps.tile([P, B], F32, name="acc%d" % i) for i in range(NT)]
+        wq_plane = sb.tile([P, L_PASSES, N], U8, name="wq_plane", align_bytes=64)
+        xq_plane = sb.tile([P, L_PASSES, B], U8, name="xq_plane", align_bytes=64)
+        result = tiles("result", [[P, B]] * N_TILES, F32)
+        acc = [ps.tile([P, B], F32, name="acc%d" % n) for n in range(N_TILES)]
 
         x_rows = xf.rearrange("(p j) t -> p j t", j=PACK)
 
         def load_x(c):
             nc.sync.dma_start(out=x_t[c][:], in_=x_rows[:, :, 2 * STARTS[c] : 2 * (STARTS[c] + WIDTHS[c])])
 
+        def load_scale_row(queue, plane, scales, r):
+            src = scales.rearrange("z (q r) n -> r q z n", r=ROWS_PER_QUADRANT)[r]
+            queue.dma_start(out=plane[r:P:32].bitcast(I32), in_=src.bitcast(I32))
+
+        def load_fp8_words(tile, words, z):
+            nc.sync.dma_start(out=tile[:].bitcast(I32), in_=words[z].rearrange("p n t -> p (n t)").bitcast(I32))
+
         def chunk_of(tile, c):
             return tile[:, PACK * STARTS[c] : PACK * (STARTS[c] + WIDTHS[c])]
 
-        def load_scale_rows(queue, plane, scales, r):
-            src = scales.rearrange("z (q r) n -> r q z n", r=4)[r]
-            queue.dma_start(out=plane[r:P:32].bitcast(I32), in_=src.bitcast(I32))
-
-        def load_words8(tile, words, z):
-            nc.sync.dma_start(out=tile[:].bitcast(I32), in_=words[z].rearrange("p n t -> p (n t)").bitcast(I32))
-
-        for plane in (xq_plane, wq_plane, wb_plane, wa_plane):
-            nc.vector.memset(plane[:].bitcast(I32), 0)
-        for plane, scales in ((xq_plane, xq_scales), (wq_plane, wq_scales), (wb_plane, wb_scales), (wa_plane, wa_scales)):
-            load_scale_rows(nc.gpsimd, plane, scales, 3)
-
-        nc.scalar.dma_start(out=fa_t[:], in_=fa.rearrange("(p j) o -> p (j o)", j=PACK))
-        nc.scalar.dma_start(out=fb_t[:], in_=fb.rearrange("(p j) o -> p (j o)", j=PACK))
-        load_x(0)
-        load_x(1)
-        load_scale_rows(nc.sync, xq_plane, xq_scales, 0)
-        load_scale_rows(nc.sync, xq_plane, xq_scales, 1)
-        load_scale_rows(nc.sync, xq_plane, xq_scales, 2)
-        load_x(2)
-        load_x(3)
-        nc.sync.dma_start(out=xq_t[:].bitcast(I32), in_=xq_words.rearrange("z p c -> p z c").bitcast(I32))
-        load_scale_rows(nc.sync, wq_plane, wq_scales, 0)
-        load_words8(wq_t[0], wq_words, 0)
-        load_scale_rows(nc.sync, wq_plane, wq_scales, 1)
-        load_scale_rows(nc.sync, wq_plane, wq_scales, 2)
-        load_x(4)
-        load_words8(wq_t[1], wq_words, 1)
-        load_words8(wb_t, wb_words, 0)
-        nc.sync.dma_start(out=wa_t[:].bitcast(I32), in_=wa_words[0].bitcast(I32))
-        load_scale_rows(nc.sync, wb_plane, wb_scales, 0)
-        load_scale_rows(nc.sync, wb_plane, wb_scales, 1)
-        load_scale_rows(nc.sync, wb_plane, wb_scales, 2)
-        load_scale_rows(nc.sync, wa_plane, wa_scales, 0)
-        load_scale_rows(nc.sync, wa_plane, wa_scales, 1)
-        load_scale_rows(nc.sync, wa_plane, wa_scales, 2)
-
         def pool_pairs(dst, c, op):
             nc.vector.tensor_tensor(out=dst[c][:], in0=x_t[c][:, :, 0::2], in1=x_t[c][:, :, 1::2], op=op)
-
-        def scale_interleave_u(c):
-            nc.vector.tensor_tensor(
-                out=chunk_of(u_in, c).rearrange("p (g i j) -> p g j i", i=2, j=PACK),
-                in0=maxes[c][:].rearrange("p j (g i) -> p g j i", i=2),
-                in1=fa_t[:].unsqueeze(1).unsqueeze(3).to_broadcast([P, WIDTHS[c] // 2, PACK, 2]),
-                op=ALU.mult,
-            )
 
         def square(c):
             nc.scalar.activation(
@@ -129,17 +89,25 @@ def tile_mix_features_pooled_over_tokens_kernel(
                 func=ACT.Square,
             )
 
-        def scale_u(c):
-            for j in range(PACK):
-                nc.scalar.activation(
-                    out=u_rows[c][:, j, :], in_=maxes[c][:, j, :], func=ACT.Copy, scale=fa_t[:, j : j + 1]
-                )
-
         def interleave_u(c):
             nc.scalar.copy(
                 out=chunk_of(u_in, c).rearrange("p (g i j) -> p g j i", i=4, j=PACK),
                 in_=u_rows[c][:].rearrange("p j (g i) -> p g j i", i=4),
             )
+
+        def scale_and_interleave_u(c):
+            nc.vector.tensor_tensor(
+                out=chunk_of(u_in, c).rearrange("p (g i j) -> p g j i", i=2, j=PACK),
+                in0=maxes[c][:].rearrange("p j (g i) -> p g j i", i=2),
+                in1=fa_t[:].unsqueeze(1).unsqueeze(3).to_broadcast([P, WIDTHS[c] // 2, PACK, 2]),
+                op=ALU.mult,
+            )
+
+        def scale_u(c):
+            for j in range(PACK):
+                nc.scalar.activation(
+                    out=u_rows[c][:, j, :], in_=maxes[c][:, j, :], func=ACT.Copy, scale=fa_t[:, j : j + 1]
+                )
 
         def scale_v(c):
             nc.vector.scalar_tensor_tensor(
@@ -151,10 +119,15 @@ def tile_mix_features_pooled_over_tokens_kernel(
                 op1=ALU.mult,
             )
 
+        def windows_completed_by(c):
+            return range(STARTS[c] // WINDOW, (STARTS[c] + WIDTHS[c]) // WINDOW)
+
         def quantize(src, codes, plane, fmt, w):
-            cols = slice(w * QW, (w + 1) * QW)
+            cols = slice(w * WINDOW, (w + 1) * WINDOW)
             nc.vector.quantize_mx(
-                out=codes[:, cols].bitcast(fmt), scales=plane[:, cols], in_=src[:, PACK * QW * w : PACK * QW * (w + 1)]
+                out=codes[:, cols].bitcast(fmt),
+                scales=plane[:, cols],
+                in_=src[:, PACK * WINDOW * w : PACK * WINDOW * (w + 1)],
             )
 
         def quantize_u(w):
@@ -163,43 +136,44 @@ def tile_mix_features_pooled_over_tokens_kernel(
         def quantize_v(w):
             quantize(v_in, v_codes, v_plane, E5M2, w)
 
-        def windows_closed_by(c):
-            return range(STARTS[c] // QW, (STARTS[c] + WIDTHS[c]) // QW)
-
-        def pass_q(n, z):
-            cols = slice(n * P, (n + 1) * P)
+        def mx_pass(n, lhsT, lhsT_plane, rhs, rhs_plane, start=False, stop=False):
             nc.tensor.matmul_mx(
                 out=acc[n][:],
-                lhsT=wq_t[z][:, cols].bitcast(E4M3),
-                lhsT_scale=wq_plane[:, z, cols],
-                rhs=xq_t[:, z, :].bitcast(E2M1),
-                rhs_scale=xq_plane[:, z, :],
-                start=(z == 0),
-                stop=False,
+                lhsT=lhsT,
+                lhsT_scale=lhsT_plane[:, n * P : (n + 1) * P],
+                rhs=rhs,
+                rhs_scale=rhs_plane,
+                start=start,
+                stop=stop,
             )
 
-        def pass_u(n):
-            nc.tensor.matmul_mx(
-                out=acc[n][:],
-                lhsT=wa_t[:, 2 * n * P : 2 * (n + 1) * P].bitcast(E2M1),
-                lhsT_scale=wa_plane[:, 0, n * P : (n + 1) * P],
-                rhs=u_codes[:].bitcast(E4M3),
-                rhs_scale=u_plane[:],
-                start=False,
-                stop=True,
-            )
+        loaded_planes = ((xq_plane, xq_scales), (wq_plane, wq_scales), (wb_plane, wb_scales), (wa_plane, wa_scales))
+        for plane, scales in loaded_planes:
+            nc.vector.memset(plane[:].bitcast(I32), 0)
 
-        def pass_v(n):
-            cols = slice(n * P, (n + 1) * P)
-            nc.tensor.matmul_mx(
-                out=acc[n][:],
-                lhsT=wb_t[:, cols].bitcast(E4M3),
-                lhsT_scale=wb_plane[:, 0, cols],
-                rhs=v_codes[:].bitcast(E5M2),
-                rhs_scale=v_plane[:],
-                start=False,
-                stop=False,
-            )
+        for plane, scales in loaded_planes:
+            load_scale_row(nc.gpsimd, plane, scales, ROWS_PER_QUADRANT - 1)
+
+        nc.scalar.dma_start(out=fa_t[:], in_=fa.rearrange("(p j) o -> p (j o)", j=PACK))
+        nc.scalar.dma_start(out=fb_t[:], in_=fb.rearrange("(p j) o -> p (j o)", j=PACK))
+        load_x(0)
+        load_x(1)
+        load_scale_row(nc.sync, xq_plane, xq_scales, 0)
+        load_scale_row(nc.sync, xq_plane, xq_scales, 1)
+        load_x(2)
+        load_x(3)
+        nc.sync.dma_start(out=xq_t[:].bitcast(I32), in_=xq_words.rearrange("z p c -> p z c").bitcast(I32))
+        load_fp8_words(wq_t[0], wq_words, 0)
+        load_scale_row(nc.sync, xq_plane, xq_scales, 2)
+        for r in range(ROWS_PER_QUADRANT - 1):
+            load_scale_row(nc.sync, wq_plane, wq_scales, r)
+        load_x(LAST)
+        load_fp8_words(wq_t[1], wq_words, 1)
+        load_fp8_words(wb_t, wb_words, 0)
+        nc.sync.dma_start(out=wa_t[:].bitcast(I32), in_=wa_words[0].bitcast(I32))
+        for plane, scales in loaded_planes[2:]:
+            for r in range(ROWS_PER_QUADRANT - 1):
+                load_scale_row(nc.sync, plane, scales, r)
 
         pool_pairs(sums, 0, ALU.add)
         pool_pairs(maxes, 0, ALU.max)
@@ -208,11 +182,11 @@ def tile_mix_features_pooled_over_tokens_kernel(
         for c in range(1, LAST):
             pool_pairs(sums, c, ALU.add)
             if c > 1:
-                for w in windows_closed_by(c - 2):
+                for w in windows_completed_by(c - 2):
                     quantize_u(w)
             scale_v(c - 1)
             pool_pairs(maxes, c, ALU.max)
-            for w in windows_closed_by(c - 1):
+            for w in windows_completed_by(c - 1):
                 quantize_v(w)
             square(c)
             interleave_u(c - 1)
@@ -221,31 +195,46 @@ def tile_mix_features_pooled_over_tokens_kernel(
         pool_pairs(maxes, LAST, ALU.max)
         square(LAST)
         interleave_u(LAST - 1)
-        for w in windows_closed_by(LAST - 2):
+        for w in windows_completed_by(LAST - 2):
             quantize_u(w)
         scale_v(LAST - 1)
-        scale_interleave_u(LAST)
+        scale_and_interleave_u(LAST)
         scale_v(LAST)
         for c in (LAST - 1, LAST):
-            for w in windows_closed_by(c):
+            for w in windows_completed_by(c):
                 quantize_v(w)
                 quantize_u(w)
 
-        for z in range(ZL):
-            for n in range(NT):
-                pass_q(n, z)
-        for n in range(NT):
-            pass_v(n)
-            pass_u(n)
+        for z in range(L_PASSES):
+            for n in range(N_TILES):
+                cols = slice(n * P, (n + 1) * P)
+                mx_pass(
+                    n,
+                    wq_t[z][:, cols].bitcast(E4M3),
+                    wq_plane[:, z, :],
+                    xq_t[:, z, :].bitcast(E2M1),
+                    xq_plane[:, z, :],
+                    start=(z == 0),
+                )
+        for n in range(N_TILES):
             rows = slice(n * P, (n + 1) * P)
+            mx_pass(n, wb_t[:, rows].bitcast(E4M3), wb_plane[:, 0, :], v_codes[:].bitcast(E5M2), v_plane[:])
+            mx_pass(
+                n,
+                wa_t[:, 2 * n * P : 2 * (n + 1) * P].bitcast(E2M1),
+                wa_plane[:, 0, :],
+                u_codes[:].bitcast(E4M3),
+                u_plane[:],
+                stop=True,
+            )
             if n == 0:
                 for h in range(2):
                     half = slice(h * B // 2, (h + 1) * B // 2)
-                    nc.scalar.copy(out=result[n][:, half], in_=acc[n][:, half])
+                    nc.vector.tensor_copy(out=result[n][:, half], in_=acc[n][:, half])
                     nc.sync.dma_start(out=out[rows, half], in_=result[n][:, half])
             elif n % 2 == 0:
-                nc.scalar.copy(out=result[n][:], in_=acc[n][:])
-                nc.scalar.dma_start(out=out[rows, :], in_=result[n][:])
-            else:
                 nc.vector.tensor_copy(out=result[n][:], in_=acc[n][:])
                 nc.sync.dma_start(out=out[rows, :], in_=result[n][:])
+            else:
+                nc.scalar.copy(out=result[n][:], in_=acc[n][:])
+                nc.scalar.dma_start(out=out[rows, :], in_=result[n][:])

from contextlib import ExitStack

import concourse.mybir as mybir

K, L, B, N = 512, 1024, 512, 512
FLOPS = 2 * N * B * (K + K + L)

F32 = mybir.dt.float32
BF16 = mybir.dt.bfloat16
I32 = mybir.dt.int32
U32 = mybir.dt.uint32
U8 = mybir.dt.uint8
E4M3 = mybir.dt.float8_e4m3fn_x4
E5M2 = mybir.dt.float8_e5m2_x4
E2M1 = mybir.dt.float4_e2m1fn_x4
ALU = mybir.AluOpType
ACT = mybir.ActivationFunctionType

P = 128
PACK = 4
ROWS_PER_QUADRANT = 4
N_TILES = N // P
L_PASSES = L // (P * PACK)

WIDTHS = (64, 96, 128, 144, 80)
STARTS = tuple(sum(WIDTHS[:c]) for c in range(len(WIDTHS)))
LAST = len(WIDTHS) - 1
WINDOW = 128


def tile_mix_features_pooled_over_tokens_kernel(
    tc, xf, fa, fb, wa_words, wa_scales, wb_words, wb_scales, xq_words, xq_scales, wq_words, wq_scales, out
):
    nc = tc.nc
    with ExitStack() as ctx:
        sb = ctx.enter_context(tc.tile_pool(name="sb", bufs=1))
        ps = ctx.enter_context(tc.psum_pool(name="ps", bufs=1))
        ctx.enter_context(tc.manual_schedule())

        def tiles(name, shapes, dtype):
            return [sb.tile(shape, dtype, name="%s%d" % (name, i), align_bytes=64) for i, shape in enumerate(shapes)]

        x_t = tiles("x_t", [[P, PACK, 2 * w] for w in WIDTHS], F32)
        fa_t = sb.tile([P, PACK], F32, name="fa_t")
        fb_t = sb.tile([P, PACK], F32, name="fb_t")
        sums = tiles("sums", [[P, PACK, w] for w in WIDTHS], F32)
        maxes = tiles("maxes", [[P, PACK, w] for w in WIDTHS], F32)
        squares = tiles("squares", [[P, w, PACK] for w in WIDTHS], F32)
        u_rows = tiles("u_rows", [[P, PACK, w] for w in WIDTHS[:LAST]], BF16)
        u_in = sb.tile([P, B * PACK], BF16, name="u_in", align_bytes=64)
        v_in = sb.tile([P, B * PACK], BF16, name="v_in", align_bytes=64)
        u_codes = sb.tile([P, B], U32, name="u_codes", align_bytes=64)
        u_plane = sb.tile([P, B], U8, name="u_plane", align_bytes=64)
        v_codes = sb.tile([P, B], U32, name="v_codes", align_bytes=64)
        v_plane = sb.tile([P, B], U8, name="v_plane", align_bytes=64)
        wa_t = sb.tile([P, 2 * N], U8, name="wa_t", align_bytes=64)
        wb_t = sb.tile([P, N], U32, name="wb_t", align_bytes=64)
        wq_t = tiles("wq_t", [[P, N]] * L_PASSES, U32)
        xq_t = sb.tile([P, L_PASSES, 2 * B], U8, name="xq_t", align_bytes=64)
        wa_plane = sb.tile([P, 1, N], U8, name="wa_plane", align_bytes=64)
        wb_plane = sb.tile([P, 1, N], U8, name="wb_plane", align_bytes=64)
        wq_plane = sb.tile([P, L_PASSES, N], U8, name="wq_plane", align_bytes=64)
        xq_plane = sb.tile([P, L_PASSES, B], U8, name="xq_plane", align_bytes=64)
        result = tiles("result", [[P, B]] * N_TILES, F32)
        acc = [ps.tile([P, B], F32, name="acc%d" % n) for n in range(N_TILES)]

        x_rows = xf.rearrange("(p j) t -> p j t", j=PACK)

        def load_x(c):
            nc.sync.dma_start(out=x_t[c][:], in_=x_rows[:, :, 2 * STARTS[c] : 2 * (STARTS[c] + WIDTHS[c])])

        def load_scale_row(queue, plane, scales, r):
            src = scales.rearrange("z (q r) n -> r q z n", r=ROWS_PER_QUADRANT)[r]
            queue.dma_start(out=plane[r:P:32].bitcast(I32), in_=src.bitcast(I32))

        def load_fp8_words(tile, words, z):
            nc.sync.dma_start(out=tile[:].bitcast(I32), in_=words[z].rearrange("p n t -> p (n t)").bitcast(I32))

        def chunk_of(tile, c):
            return tile[:, PACK * STARTS[c] : PACK * (STARTS[c] + WIDTHS[c])]

        def pool_pairs(dst, c, op):
            nc.vector.tensor_tensor(out=dst[c][:], in0=x_t[c][:, :, 0::2], in1=x_t[c][:, :, 1::2], op=op)

        def square(c):
            nc.scalar.activation(
                out=squares[c][:].rearrange("p (g i) j -> p g j i", i=2),
                in_=sums[c][:].rearrange("p j (g i) -> p g j i", i=2),
                func=ACT.Square,
            )

        def interleave_u(c):
            nc.scalar.copy(
                out=chunk_of(u_in, c).rearrange("p (g i j) -> p g j i", i=4, j=PACK),
                in_=u_rows[c][:].rearrange("p j (g i) -> p g j i", i=4),
            )

        def scale_and_interleave_u(c):
            nc.vector.tensor_tensor(
                out=chunk_of(u_in, c).rearrange("p (g i j) -> p g j i", i=2, j=PACK),
                in0=maxes[c][:].rearrange("p j (g i) -> p g j i", i=2),
                in1=fa_t[:].unsqueeze(1).unsqueeze(3).to_broadcast([P, WIDTHS[c] // 2, PACK, 2]),
                op=ALU.mult,
            )

        def scale_u(c):
            for j in range(PACK):
                nc.scalar.activation(
                    out=u_rows[c][:, j, :], in_=maxes[c][:, j, :], func=ACT.Copy, scale=fa_t[:, j : j + 1]
                )

        def scale_v(c):
            nc.vector.scalar_tensor_tensor(
                out=chunk_of(v_in, c).rearrange("p (b j) -> p b j", j=PACK),
                in0=squares[c][:],
                scalar=0.3,
                in1=fb_t[:].unsqueeze(1).to_broadcast([P, WIDTHS[c], PACK]),
                op0=ALU.mult,
                op1=ALU.mult,
            )

        def windows_completed_by(c):
            return range(STARTS[c] // WINDOW, (STARTS[c] + WIDTHS[c]) // WINDOW)

        def quantize(src, codes, plane, fmt, w):
            cols = slice(w * WINDOW, (w + 1) * WINDOW)
            nc.vector.quantize_mx(
                out=codes[:, cols].bitcast(fmt),
                scales=plane[:, cols],
                in_=src[:, PACK * WINDOW * w : PACK * WINDOW * (w + 1)],
            )

        def quantize_u(w):
            quantize(u_in, u_codes, u_plane, E4M3, w)

        def quantize_v(w):
            quantize(v_in, v_codes, v_plane, E5M2, w)

        def mx_pass(n, lhsT, lhsT_plane, rhs, rhs_plane, start=False, stop=False):
            nc.tensor.matmul_mx(
                out=acc[n][:],
                lhsT=lhsT,
                lhsT_scale=lhsT_plane[:, n * P : (n + 1) * P],
                rhs=rhs,
                rhs_scale=rhs_plane,
                start=start,
                stop=stop,
            )

        loaded_planes = ((xq_plane, xq_scales), (wq_plane, wq_scales), (wb_plane, wb_scales), (wa_plane, wa_scales))
        for plane, scales in loaded_planes:
            nc.vector.memset(plane[:].bitcast(I32), 0)

        for plane, scales in loaded_planes:
            load_scale_row(nc.gpsimd, plane, scales, ROWS_PER_QUADRANT - 1)

        nc.scalar.dma_start(out=fa_t[:], in_=fa.rearrange("(p j) o -> p (j o)", j=PACK))
        nc.scalar.dma_start(out=fb_t[:], in_=fb.rearrange("(p j) o -> p (j o)", j=PACK))
        load_x(0)
        load_x(1)
        load_scale_row(nc.sync, xq_plane, xq_scales, 0)
        load_scale_row(nc.sync, xq_plane, xq_scales, 1)
        load_x(2)
        load_x(3)
        nc.sync.dma_start(out=xq_t[:].bitcast(I32), in_=xq_words.rearrange("z p c -> p z c").bitcast(I32))
        load_fp8_words(wq_t[0], wq_words, 0)
        load_scale_row(nc.sync, xq_plane, xq_scales, 2)
        for r in range(ROWS_PER_QUADRANT - 1):
            load_scale_row(nc.sync, wq_plane, wq_scales, r)
        load_x(LAST)
        load_fp8_words(wq_t[1], wq_words, 1)
        load_fp8_words(wb_t, wb_words, 0)
        nc.sync.dma_start(out=wa_t[:].bitcast(I32), in_=wa_words[0].bitcast(I32))
        for plane, scales in loaded_planes[2:]:
            for r in range(ROWS_PER_QUADRANT - 1):
                load_scale_row(nc.sync, plane, scales, r)

        pool_pairs(sums, 0, ALU.add)
        pool_pairs(maxes, 0, ALU.max)
        square(0)
        scale_u(0)
        for c in range(1, LAST):
            pool_pairs(sums, c, ALU.add)
            if c > 1:
                for w in windows_completed_by(c - 2):
                    quantize_u(w)
            scale_v(c - 1)
            pool_pairs(maxes, c, ALU.max)
            for w in windows_completed_by(c - 1):
                quantize_v(w)
            square(c)
            interleave_u(c - 1)
            scale_u(c)
        pool_pairs(sums, LAST, ALU.add)
        pool_pairs(maxes, LAST, ALU.max)
        square(LAST)
        interleave_u(LAST - 1)
        for w in windows_completed_by(LAST - 2):
            quantize_u(w)
        scale_v(LAST - 1)
        scale_and_interleave_u(LAST)
        scale_v(LAST)
        for c in (LAST - 1, LAST):
            for w in windows_completed_by(c):
                quantize_v(w)
                quantize_u(w)

        for z in range(L_PASSES):
            for n in range(N_TILES):
                cols = slice(n * P, (n + 1) * P)
                mx_pass(
                    n,
                    wq_t[z][:, cols].bitcast(E4M3),
                    wq_plane[:, z, :],
                    xq_t[:, z, :].bitcast(E2M1),
                    xq_plane[:, z, :],
                    start=(z == 0),
                )
        for n in range(N_TILES):
            rows = slice(n * P, (n + 1) * P)
            mx_pass(n, wb_t[:, rows].bitcast(E4M3), wb_plane[:, 0, :], v_codes[:].bitcast(E5M2), v_plane[:])
            mx_pass(
                n,
                wa_t[:, 2 * n * P : 2 * (n + 1) * P].bitcast(E2M1),
                wa_plane[:, 0, :],
                u_codes[:].bitcast(E4M3),
                u_plane[:],
                stop=True,
            )
            if n == 0:
                for h in range(2):
                    half = slice(h * B // 2, (h + 1) * B // 2)
                    nc.vector.tensor_copy(out=result[n][:, half], in_=acc[n][:, half])
                    nc.sync.dma_start(out=out[rows, half], in_=result[n][:, half])
            elif n % 2 == 0:
                nc.vector.tensor_copy(out=result[n][:], in_=acc[n][:])
                nc.sync.dma_start(out=out[rows, :], in_=result[n][:])
            else:
                nc.scalar.copy(out=result[n][:], in_=acc[n][:])
                nc.scalar.dma_start(out=out[rows, :], in_=result[n][:])
